import numpy as np
import ml_dtypes


def mxq(x, axis, fmt="e4m3"):
    dtype, down = {"e4m3": (ml_dtypes.float8_e4m3fn, 7), "e5m2": (ml_dtypes.float8_e5m2, 14)}[fmt]
    v = np.moveaxis(np.asarray(x, np.float32).astype(ml_dtypes.bfloat16).astype(np.float64), axis, -1)
    blocks = v.reshape(v.shape[:-1] + (-1, 32))
    amax = np.abs(blocks).max(-1, keepdims=True)
    byte = np.maximum(np.where(amax > 0, np.frexp(amax)[1] - 1 + 127, 0) - down, 1)
    scale = np.exp2(byte - 127.0)
    codes = (blocks / scale).astype(np.float32).astype(dtype).astype(np.float64)
    return np.moveaxis((codes * scale).reshape(v.shape), -1, axis)


WIDE = False


def mx_kscale(k):
    if not WIDE:
        return np.ones(k)
    levels = np.array([10, -10, 5, -5, 0])
    if k % 512:
        return np.exp2(np.random.permutation(np.resize(levels, k // 32))).repeat(32)
    a = np.empty((k // 512, 16))
    for p in range(k // 512):
        a[p, :8] = np.random.permutation(np.resize(levels, 8))
        for g in range(8):
            far = levels[np.abs(levels - a[p, g]) >= 10]
            a[p, g + 8] = far[np.random.randint(len(far))]
    return np.exp2(a.ravel()).repeat(32)


def f64(x):
    return np.asarray(x).astype(np.float64)


def striped(idx):
    return np.tile(idx.reshape(-1, 16).T, (8, 1)).astype(np.uint16)


def unstriped(offs):
    return offs[:16].T.reshape(-1).astype(np.int64)


def striped8(idx):
    return np.concatenate([x.reshape(-1, 16).T for x in idx]).astype(np.uint16)


def runs(offs, k):
    lists = np.stack([offs[16 * r : 16 * r + 16].T.reshape(-1) for r in range(8)]).astype(np.int64)
    return lists[np.arange(k) % 512 // 64]


def pack_weight(w):
    k, n = w.shape
    w = f64(np.asarray(w, np.float32).astype(ml_dtypes.bfloat16)).reshape(k // 32, 32, n)
    amax = np.abs(w).max(1)
    byte = np.clip(np.where(amax > 0, np.frexp(amax)[1] - 1 + 127 - 7, 1), 1, 254)
    scaled = (w * np.exp2(127.0 - byte)[:, None, :]).reshape(k, n).astype(np.float32)
    words = np.ascontiguousarray(scaled.reshape(k // 512, 128, 4, n).transpose(0, 1, 3, 2)).astype(ml_dtypes.float8_e4m3fn).view(np.uint8)
    return words, np.ascontiguousarray(byte.astype(np.uint8).reshape(k // 512, 16, n))


def unpack_weight(words, scales):
    g, p, n, _ = words.shape
    vals = np.ascontiguousarray(words).view(ml_dtypes.float8_e4m3fn).astype(np.float64) * np.repeat(np.exp2(scales.astype(np.float64) - 127.0), 8, axis=1)[..., None]
    return vals.transpose(0, 1, 3, 2).reshape(g * 512, n)


def sigmoid(v):
    return 1.0 / (1.0 + np.exp(-np.maximum(v, -700.0)))

def planes(y):
    n, m = y.shape
    v = y.astype(np.float32).astype(ml_dtypes.bfloat16).astype(np.float64).reshape(n // 32, 32, m)
    top = np.abs(v).max(1)
    byte = np.clip(np.where(top > 0, np.frexp(top)[1] - 1 + 127 - 7, 1), 1, 254)
    codes = (v * np.exp2(127.0 - byte)[:, None, :]).reshape(n, m).astype(np.float32).astype(ml_dtypes.float8_e4m3fn).view(np.uint8)
    words = codes.reshape(n // 512, 128, 4, m).transpose(0, 1, 3, 2)
    return np.ascontiguousarray(words), np.ascontiguousarray(byte.astype(np.uint8).reshape(n // 512, 16, m))


K, T, S, H, J, W = 512, 2048, 512, 512, 512, 256


def setup_inputs():
    n = np.random.standard_normal
    s = mx_kscale(K)[:, None]
    u = mx_kscale(H)
    packed_xT = pack_weight(n((K, T)) * s)
    packed_w1 = pack_weight(n((K, H)) / np.sqrt(K) / s)
    packed_w2 = pack_weight(n((H, H)) / np.sqrt(H) / u[:, None])
    return {
        "x_words": packed_xT[0],
        "x_scales": packed_xT[1],
        "w1_words": packed_w1[0],
        "w1_scales": packed_w1[1],
        "tab": n((H, J)).astype(np.float32),
        "gn": (np.random.uniform(0.5, 1.5, (H, 1)) * u[:, None]).astype(np.float32),
        "w2_words": packed_w2[0],
        "w2_scales": packed_w2[1],
        "offs": striped(np.random.permutation(T)[:S]),
        "n1": striped8(np.stack([np.random.permutation(S) for _ in range(8)])),
        "n2": striped8(np.stack([np.random.permutation(S) for _ in range(8)])),
        "n3": striped8(np.random.randint(0, J, (8, S))),
        "n4": striped8(np.stack([np.random.permutation(S) for _ in range(8)])),
        "n5": striped8(np.stack([np.random.permutation(S)[:W] for _ in range(8)])),
        "n6": striped8(np.stack([np.random.permutation(S)[:W] for _ in range(8)])),
    }


def reference(x_words, x_scales, w1_words, w1_scales, tab, gn, w2_words, w2_scales, offs, n1, n2, n3, n4, n5, n6):
    xq = unpack_weight(x_words, x_scales)[:, unstriped(offs)]
    y = unpack_weight(w1_words, w1_scales).T @ xq
    z2 = f64(gn) * (np.abs(y - (y[np.arange(H)[:, None], runs(n4, H)]) - (f64(tab)[np.arange(H)[:, None], runs(n3, H)])))
    w2q = unpack_weight(w2_words, w2_scales)
    b = w2q.T @ mxq(z2, 0, "e4m3")
    st = y[np.arange(H)[:, None], runs(n1, H)] - y
    z = f64(gn) * (y * (sigmoid(st[np.arange(H)[:, None], runs(n2, H)])))
    a = w2q.T @ mxq(z, 0, "e4m3")
    ra = b[np.arange(H)[:, None], runs(n6, H)] - (0.5 * (a[np.arange(H)[:, None], runs(n5, H)]))
    out = a.copy()
    out[np.arange(H)[:, None], runs(n5, H)] = ra
    return (out,) + planes(out)

@@ -1,0 +1,200 @@
+from contextlib import ExitStack
+
+import concourse.mybir as mybir
+
+K, T, S, H, W = 512, 2048, 512, 512, 256
+FLOPS = 3 * 2 * K * H * S
+
+F32 = mybir.dt.float32
+BF16 = mybir.dt.bfloat16
+I32 = mybir.dt.int32
+U32 = mybir.dt.uint32
+U16 = mybir.dt.uint16
+U8 = mybir.dt.uint8
+FP8X4 = mybir.dt.float8_e4m3fn_x4
+ALU = mybir.AluOpType
+ACT = mybir.ActivationFunctionType
+
+P = 128
+PACK = 4
+WINDOW = 2 * S
+
+
+def as_words(dram):
+    return dram[0].rearrange("p n t -> p (n t)").bitcast(I32)
+
+
+def load_scale_rows(queue, tile, dram):
+    for q in range(4):
+        queue.dma_start(out=tile[32 * q : 32 * q + 4, :].bitcast(I32), in_=dram[0, 4 * q : 4 * q + 4, :].bitcast(I32))
+
+
+def side_by_side(packed):
+    return packed.rearrange("p (c i t) -> p c t i", i=2, t=PACK)
+
+
+def by_planes(planes):
+    return planes.rearrange("p t (c i) -> p c t i", i=2)
+
+
+def tile_picked_tieputbhopdkindd_none_po_kernel(
+    tc, x_words, x_scales, w1_words, w1_scales, tab, gn, w2_words, w2_scales, offs, n1, n2, n3, n4, n5, n6, out_0, out_1, out_2
+):
+    nc = tc.nc
+    with ExitStack() as ctx:
+        keep = ctx.enter_context(tc.tile_pool(name="keep", bufs=1))
+        psum = ctx.enter_context(tc.psum_pool(name="psum", bufs=1))
+
+        def sb(name, shape, dtype):
+            return keep.tile(shape, dtype, name=name, align_bytes=64)
+
+        def load_list(name, dram):
+            tile = keep.tile(list(dram.shape), U16, name=name)
+            nc.sync.dma_start(tile[:], dram)
+            return tile
+
+        x_scale_rows = sb("x_scale_rows", [P, T], U8)
+        w1_scale_rows = sb("w1_scale_rows", [P, H], U8)
+        w2_scale_rows = sb("w2_scale_rows", [P, H], U8)
+        nc.vector.memset(x_scale_rows[:].bitcast(I32), 0)
+        nc.gpsimd.memset(w1_scale_rows[:].bitcast(I32), 0)
+        nc.gpsimd.memset(w2_scale_rows[:].bitcast(I32), 0)
+        load_scale_rows(nc.scalar, x_scale_rows, x_scales)
+        load_scale_rows(nc.gpsimd, w1_scale_rows, w1_scales)
+
+        x_codes = sb("x_codes", [P, T], U32)
+        nc.sync.dma_start(out=x_codes[:].bitcast(I32), in_=as_words(x_words))
+        offs_sb = load_list("offs_sb", offs)
+        w1_raw = sb("w1_raw", [P, H], I32)
+        nc.sync.dma_start(out=w1_raw[:], in_=as_words(w1_words))
+        tab_rows = tab.rearrange("(p t) j -> p t j", t=PACK)
+        tab_win = [sb(f"tab_win{t}", [P, WINDOW], F32) for t in range(PACK)]
+        nc.sync.dma_start(out=tab_win[0][:, :S], in_=tab_rows[:, 0, :])
+        n3_sb = load_list("n3_sb", n3)
+        w2_raw = sb("w2_raw", [P, H], I32)
+        nc.sync.dma_start(out=w2_raw[:], in_=as_words(w2_words))
+        n1_sb = load_list("n1_sb", n1)
+        gain = sb("gain", [P, PACK], F32)
+        nc.sync.dma_start(out=gain[:], in_=gn.rearrange("(p t) o -> p (t o)", t=PACK))
+        for t in range(1, PACK):
+            nc.sync.dma_start(out=tab_win[t][:, :S], in_=tab_rows[:, t, :])
+        load_scale_rows(nc.sync, w2_scale_rows, w2_scales)
+        n4_sb = load_list("n4_sb", n4)
+        n2_sb = load_list("n2_sb", n2)
+        n5_sb = load_list("n5_sb", n5)
+        n6_sb = load_list("n6_sb", n6)
+
+        def deal(name, raw, dtype):
+            dealt = sb(name, [P, H], dtype)
+            nc.vector.tensor_copy(
+                out=dealt[:].rearrange("p (t m) -> p t m", t=PACK), in_=raw[:].rearrange("p (m t) -> p t m", t=PACK)
+            )
+            return dealt
+
+        picked_scales = sb("picked_scales", [P, S], U8)
+        picked_codes = sb("picked_codes", [P, S], U32)
+        nc.vector.tensor_copy(picked_scales[:], x_scale_rows[:].indirect(offs_sb[:]))
+        nc.vector.tensor_copy(picked_codes[:], x_codes[:].indirect(offs_sb[:]))
+        w1_scale = deal("w1_scale", w1_scale_rows, U8)
+        w1_codes = deal("w1_codes", w1_raw, I32)
+
+        def product(tag, w_codes, w_scale, codes, scales):
+            banks = []
+            for t in range(PACK):
+                bank = psum.tile([P, S], F32, name=f"{tag}{t}")
+                cols = slice(t * P, (t + 1) * P)
+                nc.tensor.matmul_mx(
+                    out=bank[:],
+                    lhsT=w_codes[:, cols].bitcast(FP8X4),
+                    lhsT_scale=w_scale[:, cols],
+                    rhs=codes[:].bitcast(FP8X4),
+                    rhs_scale=scales[:],
+                    start=True,
+                    stop=True,
+                )
+                banks.append(bank)
+            return banks
+
+        y_banks = product("first", w1_codes, w1_scale, picked_codes, picked_scales)
+        w2_scale = deal("w2_scale", w2_scale_rows, U8)
+        w2_codes = deal("w2_codes", w2_raw, I32)
+
+        y_plain = sb("y_plain", [P, PACK, S], F32)
+        y_win = [sb(f"y_win{t}", [P, WINDOW], F32) for t in range(PACK)]
+        gained_y = sb("gained_y", [P, PACK, S], F32)
+        for t in range(PACK):
+            nc.scalar.copy(y_plain[:, t, :], y_banks[t][:])
+            nc.scalar.copy(y_win[t][:, :S], y_banks[t][:])
+        for t in range(PACK):
+            nc.scalar.activation(gained_y[:, t, :], y_banks[t][:], ACT.Copy, scale=gain[:, t : t + 1])
+
+        tab_less_y = sb("tab_less_y", [P, PACK, S], F32)
+        st_win = [sb(f"st_win{t}", [P, WINDOW], F32) for t in range(PACK)]
+        gate = sb("gate", [P, PACK, S], F32)
+        for t in range(PACK):
+            nc.vector.tensor_tensor(tab_less_y[:, t, :], tab_win[t][:].indirect(n3_sb[:]), y_plain[:, t, :], ALU.subtract)
+            nc.vector.tensor_tensor(st_win[t][:, :S], y_win[t][:].indirect(n1_sb[:]), y_plain[:, t, :], ALU.subtract)
+        for t in range(PACK):
+            nc.scalar.activation(gate[:, t, :], st_win[t][:].indirect(n2_sb[:]), ACT.Sigmoid)
+
+        diff = sb("diff", [P, PACK, S], F32)
+        size = sb("size", [P, PACK, S], F32)
+        z2 = sb("z2", [P, PACK, S], F32)
+
+        def z2_plane(t):
+            nc.vector.tensor_tensor(diff[:, t, :], y_win[t][:].indirect(n4_sb[:]), tab_less_y[:, t, :], ALU.add)
+            nc.scalar.activation(size[:, t, :], diff[:, t, :], ACT.Abs)
+            nc.scalar.activation(z2[:, t, :], size[:, t, :], ACT.Copy, scale=gain[:, t : t + 1])
+
+        def quantize(name, packed):
+            codes = sb(name + "_codes", [P, S], U32)
+            scales = sb(name + "_scales", [P, S], U8)
+            nc.vector.quantize_mx(out=codes[:].bitcast(FP8X4), scales=scales[:], in_=packed[:])
+            return codes, scales
+
+        z2_plane(0)
+        z2_plane(1)
+        z_packed = sb("z_packed", [P, PACK * S], BF16)
+        nc.vector.tensor_tensor(side_by_side(z_packed[:]), by_planes(gate[:]), by_planes(gained_y[:]), ALU.mult)
+        z_codes, z_scales = quantize("z", z_packed)
+        a_banks = product("second", w2_codes, w2_scale, z_codes, z_scales)
+        z2_plane(2)
+        z2_plane(3)
+
+        result = [sb(f"result{t}", [P, S], F32) for t in range(PACK)]
+        half_a = sb("half_a", [P, PACK, W], F32)
+        for t in range(PACK):
+            nc.scalar.copy(result[t][:], a_banks[t][:])
+
+        def fetch_a(t):
+            nc.vector.tensor_scalar(half_a[:, t, :], result[t][:].indirect(n5_sb[:]), -0.5, 0.0, ALU.mult, ALU.add)
+
+        fetch_a(0)
+        z2_packed = sb("z2_packed", [P, PACK * S], BF16)
+        nc.vector.tensor_copy(side_by_side(z2_packed[:]), by_planes(z2[:]))
+        fetch_a(1)
+        z2_codes, z2_scales = quantize("z2", z2_packed)
+        b_banks = product("first", w2_codes, w2_scale, z2_codes, z2_scales)
+        fetch_a(2)
+        fetch_a(3)
+
+        b_win = [sb(f"b_win{t}", [P, S], F32) for t in range(PACK)]
+        picked_b = sb("picked_b", [P, PACK, W], F32)
+        out_rows = out_0.rearrange("(p t) j -> p t j", t=PACK)
+        for t in range(PACK):
+            nc.scalar.copy(b_win[t][:], b_banks[t][:])
+            nc.vector.tensor_copy(picked_b[:, t, :], b_win[t][:].indirect(n6_sb[:]))
+            nc.vector.tensor_tensor(result[t][:].indirect(n5_sb[:]), picked_b[:, t, :], half_a[:, t, :], ALU.add)
+            nc.sync.dma_start(out=out_rows[:, t, :], in_=result[t][:])
+
+        rounded = sb("rounded", [P, PACK, S], BF16)
+        for t in range(PACK - 1):
+            nc.scalar.copy(rounded[:, t, :], result[t][:])
+        nc.vector.tensor_copy(rounded[:, PACK - 1, :], result[PACK - 1][:])
+        out_packed = sb("out_packed", [P, PACK * S], BF16)
+        nc.vector.tensor_copy(side_by_side(out_packed[:]), by_planes(rounded[:]))
+        out_codes, out_scales = quantize("out", out_packed)
+        nc.sync.dma_start(out=as_words(out_1), in_=out_codes[:].bitcast(I32))
+        for q in range(4):
+            queue = nc.scalar if q % 2 else nc.sync
+            queue.dma_start(out=out_2[0, 4 * q : 4 * q + 4, :].bitcast(I32), in_=out_scales[32 * q : 32 * q + 4, :].bitcast(I32))

@@ -24,17 +24,24 @@ def as_words(dram):
     return dram[0].rearrange("p n t -> p (n t)").bitcast(I32)
 
 
-def load_scale_rows(queue, tile, dram):
-    for q in range(4):
+def load_scale_rows(queue, tile, dram, quadrants=range(4)):
+    for q in quadrants:
         queue.dma_start(out=tile[32 * q : 32 * q + 4, :].bitcast(I32), in_=dram[0, 4 * q : 4 * q + 4, :].bitcast(I32))
 
 
-def side_by_side(packed):
-    return packed.rearrange("p (c i t) -> p c t i", i=2, t=PACK)
+HALVES = (slice(0, S // 2), slice(S // 2, S))
 
 
-def by_planes(planes):
-    return planes.rearrange("p t (c i) -> p c t i", i=2)
+def packed_cols(cols):
+    return slice(PACK * cols.start, PACK * cols.stop)
+
+
+def side_by_side(packed, cols):
+    return packed[:, packed_cols(cols)].rearrange("p (c i t) -> p c t i", i=2, t=PACK)
+
+
+def by_planes(planes, cols):
+    return planes[:, :, cols].rearrange("p t (c i) -> p c t i", i=2)
 
 
 def tile_picked_tieputbhopdkindd_none_po_kernel(
@@ -45,8 +52,8 @@ def tile_picked_tieputbhopdkindd_none_po_kernel(
         keep = ctx.enter_context(tc.tile_pool(name="keep", bufs=1))
         psum = ctx.enter_context(tc.psum_pool(name="psum", bufs=1))
 
-        def sb(name, shape, dtype):
-            return keep.tile(shape, dtype, name=name, align_bytes=64)
+        def sb(name, shape, dtype, tag=None):
+            return keep.tile(shape, dtype, name=name, tag=tag or name, align_bytes=64)
 
         def load_list(name, dram):
             tile = keep.tile(list(dram.shape), U16, name=name)
@@ -56,145 +63,179 @@ def tile_picked_tieputbhopdkindd_none_po_kernel(
         x_scale_rows = sb("x_scale_rows", [P, T], U8)
         w1_scale_rows = sb("w1_scale_rows", [P, H], U8)
         w2_scale_rows = sb("w2_scale_rows", [P, H], U8)
-        nc.vector.memset(x_scale_rows[:].bitcast(I32), 0)
-        nc.gpsimd.memset(w1_scale_rows[:].bitcast(I32), 0)
-        nc.gpsimd.memset(w2_scale_rows[:].bitcast(I32), 0)
-        load_scale_rows(nc.scalar, x_scale_rows, x_scales)
-        load_scale_rows(nc.gpsimd, w1_scale_rows, w1_scales)
+        nc.vector.memset(x_scale_rows[:, : T // 2].bitcast(I32), 0)
+        nc.gpsimd.memset(x_scale_rows[:, T // 2 :].bitcast(I32), 0)
+        nc.vector.memset(w1_scale_rows[:].bitcast(I32), 0)
+        nc.vector.memset(w2_scale_rows[:].bitcast(I32), 0)
+        minus_half = sb("minus_half", [P, W], F32)
+        nc.vector.memset(minus_half[:], -0.5)
 
+        load_scale_rows(nc.sync, x_scale_rows, x_scales, range(0, 2))
+        load_scale_rows(nc.scalar, x_scale_rows, x_scales, range(2, 4))
+        load_scale_rows(nc.scalar, w1_scale_rows, w1_scales, range(0, 2))
+        offs_sb = load_list("offs_sb", offs)
         x_codes = sb("x_codes", [P, T], U32)
         nc.sync.dma_start(out=x_codes[:].bitcast(I32), in_=as_words(x_words))
-        offs_sb = load_list("offs_sb", offs)
+        load_scale_rows(nc.sync, w1_scale_rows, w1_scales, range(2, 4))
         w1_raw = sb("w1_raw", [P, H], I32)
         nc.sync.dma_start(out=w1_raw[:], in_=as_words(w1_words))
+        w2_raw = sb("w2_raw", [P, H], I32)
+        nc.sync.dma_start(out=w2_raw[:], in_=as_words(w2_words))
         tab_rows = tab.rearrange("(p t) j -> p t j", t=PACK)
         tab_win = [sb(f"tab_win{t}", [P, WINDOW], F32) for t in range(PACK)]
         nc.sync.dma_start(out=tab_win[0][:, :S], in_=tab_rows[:, 0, :])
         n3_sb = load_list("n3_sb", n3)
-        w2_raw = sb("w2_raw", [P, H], I32)
-        nc.sync.dma_start(out=w2_raw[:], in_=as_words(w2_words))
+        load_scale_rows(nc.sync, w2_scale_rows, w2_scales)
         n1_sb = load_list("n1_sb", n1)
+        n4_sb = load_list("n4_sb", n4)
         gain = sb("gain", [P, PACK], F32)
         nc.sync.dma_start(out=gain[:], in_=gn.rearrange("(p t) o -> p (t o)", t=PACK))
+        n2_sb = load_list("n2_sb", n2)
         for t in range(1, PACK):
             nc.sync.dma_start(out=tab_win[t][:, :S], in_=tab_rows[:, t, :])
-        load_scale_rows(nc.sync, w2_scale_rows, w2_scales)
-        n4_sb = load_list("n4_sb", n4)
-        n2_sb = load_list("n2_sb", n2)
         n5_sb = load_list("n5_sb", n5)
         n6_sb = load_list("n6_sb", n6)
+        warm = sb("warm", [P, 1], F32)
+        nc.scalar.activation(warm[:], minus_half[:, 0:1], ACT.Sigmoid)
 
-        def deal(name, raw, dtype):
-            dealt = sb(name, [P, H], dtype)
+        def deal(dealt, raw, tiles):
             nc.vector.tensor_copy(
-                out=dealt[:].rearrange("p (t m) -> p t m", t=PACK), in_=raw[:].rearrange("p (m t) -> p t m", t=PACK)
+                out=dealt[:].rearrange("p (t m) -> p m t", t=PACK)[:, :, tiles],
+                in_=raw[:].rearrange("p (m t) -> p m t", t=PACK)[:, :, tiles],
             )
-            return dealt
 
         picked_scales = sb("picked_scales", [P, S], U8)
         picked_codes = sb("picked_codes", [P, S], U32)
+        w1_codes, w2_codes = sb("w1_codes", [P, H], I32), sb("w2_codes", [P, H], I32)
         nc.vector.tensor_copy(picked_scales[:], x_scale_rows[:].indirect(offs_sb[:]))
         nc.vector.tensor_copy(picked_codes[:], x_codes[:].indirect(offs_sb[:]))
-        w1_scale = deal("w1_scale", w1_scale_rows, U8)
-        w1_codes = deal("w1_codes", w1_raw, I32)
+        w1_scale = sb("w1_scale", [P, H], U8, tag="x_codes")
+        for tiles in (slice(0, 1), slice(1, PACK)):
+            deal(w1_codes, w1_raw, tiles)
+            deal(w1_scale, w1_scale_rows, tiles)
 
-        def product(tag, w_codes, w_scale, codes, scales):
-            banks = []
-            for t in range(PACK):
-                bank = psum.tile([P, S], F32, name=f"{tag}{t}")
-                cols = slice(t * P, (t + 1) * P)
-                nc.tensor.matmul_mx(
-                    out=bank[:],
-                    lhsT=w_codes[:, cols].bitcast(FP8X4),
-                    lhsT_scale=w_scale[:, cols],
-                    rhs=codes[:].bitcast(FP8X4),
-                    rhs_scale=scales[:],
-                    start=True,
-                    stop=True,
-                )
-                banks.append(bank)
-            return banks
+        def product(tag, t, w_codes, w_scale, codes, scales, places=slice(0, S)):
+            bank = psum.tile([P, places.stop - places.start], F32, name=tag)
+            cols = slice(t * P, (t + 1) * P)
+            nc.tensor.matmul_mx(
+                out=bank[:],
+                lhsT=w_codes[:, cols].bitcast(FP8X4),
+                lhsT_scale=w_scale[:, cols],
+                rhs=codes[:, places].bitcast(FP8X4),
+                rhs_scale=scales[:, places],
+                start=True,
+                stop=True,
+            )
+            return bank
 
-        y_banks = product("first", w1_codes, w1_scale, picked_codes, picked_scales)
-        w2_scale = deal("w2_scale", w2_scale_rows, U8)
-        w2_codes = deal("w2_codes", w2_raw, I32)
+        y_pieces = [[(PACK, HALVES[0]), (0, HALVES[1])]] + [[(t, slice(0, S))] for t in range(1, PACK)]
+        y_banks = [
+            [(product(f"bank{number}", t, w1_codes, w1_scale, picked_codes, picked_scales, places), places) for number, places in pieces]
+            for t, pieces in enumerate(y_pieces)
+        ]
+        deal(w2_codes, w2_raw, slice(0, PACK))
+        w2_scale = sb("w2_scale", [P, H], U8)
+        deal(w2_scale, w2_scale_rows, slice(0, PACK))
 
         y_plain = sb("y_plain", [P, PACK, S], F32)
         y_win = [sb(f"y_win{t}", [P, WINDOW], F32) for t in range(PACK)]
         gained_y = sb("gained_y", [P, PACK, S], F32)
         for t in range(PACK):
-            nc.scalar.copy(y_plain[:, t, :], y_banks[t][:])
-            nc.scalar.copy(y_win[t][:, :S], y_banks[t][:])
+            copies = (y_plain[:, t, :], y_win[t][:, :S])
+            for copy_of_y in copies if t < PACK - 1 else reversed(copies):
+                for bank, places in y_banks[t]:
+                    nc.scalar.copy(copy_of_y[:, places], bank[:])
         for t in range(PACK):
-            nc.scalar.activation(gained_y[:, t, :], y_banks[t][:], ACT.Copy, scale=gain[:, t : t + 1])
+            for bank, places in y_banks[t]:
+                nc.scalar.activation(gained_y[:, t, places], bank[:], ACT.Copy, scale=gain[:, t : t + 1])
 
         tab_less_y = sb("tab_less_y", [P, PACK, S], F32)
         st_win = [sb(f"st_win{t}", [P, WINDOW], F32) for t in range(PACK)]
         gate = sb("gate", [P, PACK, S], F32)
-        for t in range(PACK):
-            nc.vector.tensor_tensor(tab_less_y[:, t, :], tab_win[t][:].indirect(n3_sb[:]), y_plain[:, t, :], ALU.subtract)
-            nc.vector.tensor_tensor(st_win[t][:, :S], y_win[t][:].indirect(n1_sb[:]), y_plain[:, t, :], ALU.subtract)
-        for t in range(PACK):
-            nc.scalar.activation(gate[:, t, :], st_win[t][:].indirect(n2_sb[:]), ACT.Sigmoid)
-
-        diff = sb("diff", [P, PACK, S], F32)
         size = sb("size", [P, PACK, S], F32)
         z2 = sb("z2", [P, PACK, S], F32)
 
-        def z2_plane(t):
-            nc.vector.tensor_tensor(diff[:, t, :], y_win[t][:].indirect(n4_sb[:]), tab_less_y[:, t, :], ALU.add)
-            nc.scalar.activation(size[:, t, :], diff[:, t, :], ACT.Abs)
+        def differences(t):
+            nc.vector.tensor_tensor(tab_less_y[:, t, :], tab_win[t][:].indirect(n3_sb[:]), y_plain[:, t, :], ALU.subtract)
+            nc.vector.tensor_tensor(st_win[t][:, :S], y_win[t][:].indirect(n1_sb[:]), y_plain[:, t, :], ALU.subtract)
+            nc.scalar.activation(gate[:, t, :], st_win[t][:].indirect(n2_sb[:]), ACT.Sigmoid)
+
+        def z2_plane(t, tag):
+            diff = sb(f"diff{t}", [P, S], F32, tag=tag)
+            nc.vector.tensor_tensor(diff[:], y_win[t][:].indirect(n4_sb[:]), tab_less_y[:, t, :], ALU.add)
+            nc.scalar.activation(size[:, t, :], diff[:], ACT.Abs)
             nc.scalar.activation(z2[:, t, :], size[:, t, :], ACT.Copy, scale=gain[:, t : t + 1])
+
+        for t in range(PACK - 2):
+            differences(t)
+            z2_plane(t, None)
+        differences(2)
+        differences(3)
+        z2_plane(2, "tab_win3")
+        z2_plane(3, None)
 
         def quantize(name, packed):
             codes = sb(name + "_codes", [P, S], U32)
             scales = sb(name + "_scales", [P, S], U8)
-            nc.vector.quantize_mx(out=codes[:].bitcast(FP8X4), scales=scales[:], in_=packed[:])
+            for cols in HALVES:
+                nc.vector.quantize_mx(out=codes[:, cols].bitcast(FP8X4), scales=scales[:, cols], in_=packed[:, packed_cols(cols)])
             return codes, scales
 
-        z2_plane(0)
-        z2_plane(1)
         z_packed = sb("z_packed", [P, PACK * S], BF16)
-        nc.vector.tensor_tensor(side_by_side(z_packed[:]), by_planes(gate[:]), by_planes(gained_y[:]), ALU.mult)
+        for cols in HALVES:
+            nc.vector.tensor_tensor(side_by_side(z_packed, cols), by_planes(gate, cols), by_planes(gained_y, cols), ALU.mult)
         z_codes, z_scales = quantize("z", z_packed)
-        a_banks = product("second", w2_codes, w2_scale, z_codes, z_scales)
-        z2_plane(2)
-        z2_plane(3)
+        z2_packed = sb("z2_packed", [P, PACK * S], BF16)
+        nc.scalar.copy(side_by_side(z2_packed, HALVES[0]), by_planes(z2, HALVES[0]))
+        nc.vector.tensor_copy(side_by_side(z2_packed, HALVES[1]), by_planes(z2, HALVES[1]))
+        z2_codes, z2_scales = quantize("z2", z2_packed)
 
         result = [sb(f"result{t}", [P, S], F32) for t in range(PACK)]
-        half_a = sb("half_a", [P, PACK, W], F32)
-        for t in range(PACK):
-            nc.scalar.copy(result[t][:], a_banks[t][:])
-
-        def fetch_a(t):
-            nc.vector.tensor_scalar(half_a[:, t, :], result[t][:].indirect(n5_sb[:]), -0.5, 0.0, ALU.mult, ALU.add)
-
-        fetch_a(0)
-        z2_packed = sb("z2_packed", [P, PACK * S], BF16)
-        nc.vector.tensor_copy(side_by_side(z2_packed[:]), by_planes(z2[:]))
-        fetch_a(1)
-        z2_codes, z2_scales = quantize("z2", z2_packed)
-        b_banks = product("first", w2_codes, w2_scale, z2_codes, z2_scales)
-        fetch_a(2)
-        fetch_a(3)
-
         b_win = [sb(f"b_win{t}", [P, S], F32) for t in range(PACK)]
+        half_a = sb("half_a", [P, PACK, W], F32)
         picked_b = sb("picked_b", [P, PACK, W], F32)
         out_rows = out_0.rearrange("(p t) j -> p t j", t=PACK)
-        for t in range(PACK):
-            nc.scalar.copy(b_win[t][:], b_banks[t][:])
-            nc.vector.tensor_copy(picked_b[:, t, :], b_win[t][:].indirect(n6_sb[:]))
-            nc.vector.tensor_tensor(result[t][:].indirect(n5_sb[:]), picked_b[:, t, :], half_a[:, t, :], ALU.add)
-            nc.sync.dma_start(out=out_rows[:, t, :], in_=result[t][:])
-
-        rounded = sb("rounded", [P, PACK, S], BF16)
-        for t in range(PACK - 1):
-            nc.scalar.copy(rounded[:, t, :], result[t][:])
-        nc.vector.tensor_copy(rounded[:, PACK - 1, :], result[PACK - 1][:])
         out_packed = sb("out_packed", [P, PACK * S], BF16)
-        nc.vector.tensor_copy(side_by_side(out_packed[:]), by_planes(rounded[:]))
+        out_slots = out_packed[:].rearrange("p (c t) -> p t c", t=PACK)
+
+        def make_a(t):
+            pieces = [(PACK + t, slice(0, S))] if t > 0 else [(PACK - 1, HALVES[0]), (PACK, HALVES[1])]
+            for number, places in pieces:
+                bank = product(f"bank{number}", t, w2_codes, w2_scale, z_codes, z_scales, places)
+                nc.scalar.copy(result[t][:, places], bank[:])
+
+        def make_b(t):
+            bank = product(f"bank{t}", t, w2_codes, w2_scale, z2_codes, z2_scales)
+            nc.scalar.activation(b_win[t][:], bank[:], ACT.Copy, scale=-2.0)
+
+        def fetch_a(t):
+            nc.vector.tensor_copy(half_a[:, t, :], result[t][:].indirect(n5_sb[:]))
+
+        def fetch_b(t):
+            nc.vector.tensor_tensor(picked_b[:, t, :], b_win[t][:].indirect(n6_sb[:]), half_a[:, t, :], ALU.add)
+
+        def put_back(t):
+            nc.vector.tensor_tensor(result[t][:].indirect(n5_sb[:]), picked_b[:, t, :], minus_half[:], ALU.mult)
+            nc.sync.dma_start(out=out_rows[:, t, :], in_=result[t][:])
+            scalar_cols = slice(0, S) if t < 2 else HALVES[1]
+            nc.scalar.copy(out_slots[:, t, scalar_cols], result[t][:, scalar_cols])
+
+        for t in range(PACK):
+            make_a(t)
+            fetch_a(t)
+        for t in range(PACK):
+            make_b(t)
+        for t in range(PACK):
+            fetch_b(t)
+            if t > 0:
+                put_back(t - 1)
+        put_back(PACK - 1)
+        for t in (2, 3):
+            nc.vector.tensor_copy(out_slots[:, t, HALVES[0]], result[t][:, HALVES[0]])
+
         out_codes, out_scales = quantize("out", out_packed)
-        nc.sync.dma_start(out=as_words(out_1), in_=out_codes[:].bitcast(I32))
+        for cols, queue in zip(HALVES, (nc.sync, nc.scalar)):
+            queue.dma_start(out=as_words(out_1)[:, cols], in_=out_codes[:, cols].bitcast(I32))
         for q in range(4):
             queue = nc.scalar if q % 2 else nc.sync
             queue.dma_start(out=out_2[0, 4 * q : 4 * q + 4, :].bitcast(I32), in_=out_scales[32 * q : 32 * q + 4, :].bitcast(I32))

from contextlib import ExitStack

import concourse.mybir as mybir

K, T, S, H, W = 512, 2048, 512, 512, 256
FLOPS = 3 * 2 * K * H * S

F32 = mybir.dt.float32
BF16 = mybir.dt.bfloat16
I32 = mybir.dt.int32
U32 = mybir.dt.uint32
U16 = mybir.dt.uint16
U8 = mybir.dt.uint8
FP8X4 = mybir.dt.float8_e4m3fn_x4
ALU = mybir.AluOpType
ACT = mybir.ActivationFunctionType

P = 128
PACK = 4
WINDOW = 2 * S


def as_words(dram):
    return dram[0].rearrange("p n t -> p (n t)").bitcast(I32)


def load_scale_rows(queue, tile, dram, quadrants=range(4)):
    for q in quadrants:
        queue.dma_start(out=tile[32 * q : 32 * q + 4, :].bitcast(I32), in_=dram[0, 4 * q : 4 * q + 4, :].bitcast(I32))


HALVES = (slice(0, S // 2), slice(S // 2, S))


def packed_cols(cols):
    return slice(PACK * cols.start, PACK * cols.stop)


def side_by_side(packed, cols):
    return packed[:, packed_cols(cols)].rearrange("p (c i t) -> p c t i", i=2, t=PACK)


def by_planes(planes, cols):
    return planes[:, :, cols].rearrange("p t (c i) -> p c t i", i=2)


def tile_picked_tieputbhopdkindd_none_po_kernel(
    tc, x_words, x_scales, w1_words, w1_scales, tab, gn, w2_words, w2_scales, offs, n1, n2, n3, n4, n5, n6, out_0, out_1, out_2
):
    nc = tc.nc
    with ExitStack() as ctx:
        keep = ctx.enter_context(tc.tile_pool(name="keep", bufs=1))
        psum = ctx.enter_context(tc.psum_pool(name="psum", bufs=1))

        def sb(name, shape, dtype, tag=None):
            return keep.tile(shape, dtype, name=name, tag=tag or name, align_bytes=64)

        def load_list(name, dram):
            tile = keep.tile(list(dram.shape), U16, name=name)
            nc.sync.dma_start(tile[:], dram)
            return tile

        x_scale_rows = sb("x_scale_rows", [P, T], U8)
        w1_scale_rows = sb("w1_scale_rows", [P, H], U8)
        w2_scale_rows = sb("w2_scale_rows", [P, H], U8)
        nc.vector.memset(x_scale_rows[:, : T // 2].bitcast(I32), 0)
        nc.gpsimd.memset(x_scale_rows[:, T // 2 :].bitcast(I32), 0)
        nc.vector.memset(w1_scale_rows[:].bitcast(I32), 0)
        nc.vector.memset(w2_scale_rows[:].bitcast(I32), 0)
        minus_half = sb("minus_half", [P, W], F32)
        nc.vector.memset(minus_half[:], -0.5)

        load_scale_rows(nc.sync, x_scale_rows, x_scales, range(0, 2))
        load_scale_rows(nc.scalar, x_scale_rows, x_scales, range(2, 4))
        load_scale_rows(nc.scalar, w1_scale_rows, w1_scales, range(0, 2))
        offs_sb = load_list("offs_sb", offs)
        x_codes = sb("x_codes", [P, T], U32)
        nc.sync.dma_start(out=x_codes[:].bitcast(I32), in_=as_words(x_words))
        load_scale_rows(nc.sync, w1_scale_rows, w1_scales, range(2, 4))
        w1_raw = sb("w1_raw", [P, H], I32)
        nc.sync.dma_start(out=w1_raw[:], in_=as_words(w1_words))
        w2_raw = sb("w2_raw", [P, H], I32)
        nc.sync.dma_start(out=w2_raw[:], in_=as_words(w2_words))
        tab_rows = tab.rearrange("(p t) j -> p t j", t=PACK)
        tab_win = [sb(f"tab_win{t}", [P, WINDOW], F32) for t in range(PACK)]
        nc.sync.dma_start(out=tab_win[0][:, :S], in_=tab_rows[:, 0, :])
        n3_sb = load_list("n3_sb", n3)
        load_scale_rows(nc.sync, w2_scale_rows, w2_scales)
        n1_sb = load_list("n1_sb", n1)
        n4_sb = load_list("n4_sb", n4)
        gain = sb("gain", [P, PACK], F32)
        nc.sync.dma_start(out=gain[:], in_=gn.rearrange("(p t) o -> p (t o)", t=PACK))
        n2_sb = load_list("n2_sb", n2)
        for t in range(1, PACK):
            nc.sync.dma_start(out=tab_win[t][:, :S], in_=tab_rows[:, t, :])
        n5_sb = load_list("n5_sb", n5)
        n6_sb = load_list("n6_sb", n6)
        warm = sb("warm", [P, 1], F32)
        nc.scalar.activation(warm[:], minus_half[:, 0:1], ACT.Sigmoid)

        def deal(dealt, raw, tiles):
            nc.vector.tensor_copy(
                out=dealt[:].rearrange("p (t m) -> p m t", t=PACK)[:, :, tiles],
                in_=raw[:].rearrange("p (m t) -> p m t", t=PACK)[:, :, tiles],
            )

        picked_scales = sb("picked_scales", [P, S], U8)
        picked_codes = sb("picked_codes", [P, S], U32)
        w1_codes, w2_codes = sb("w1_codes", [P, H], I32), sb("w2_codes", [P, H], I32)
        nc.vector.tensor_copy(picked_scales[:], x_scale_rows[:].indirect(offs_sb[:]))
        nc.vector.tensor_copy(picked_codes[:], x_codes[:].indirect(offs_sb[:]))
        w1_scale = sb("w1_scale", [P, H], U8, tag="x_codes")
        for tiles in (slice(0, 1), slice(1, PACK)):
            deal(w1_codes, w1_raw, tiles)
            deal(w1_scale, w1_scale_rows, tiles)

        def product(tag, t, w_codes, w_scale, codes, scales, places=slice(0, S)):
            bank = psum.tile([P, places.stop - places.start], F32, name=tag)
            cols = slice(t * P, (t + 1) * P)
            nc.tensor.matmul_mx(
                out=bank[:],
                lhsT=w_codes[:, cols].bitcast(FP8X4),
                lhsT_scale=w_scale[:, cols],
                rhs=codes[:, places].bitcast(FP8X4),
                rhs_scale=scales[:, places],
                start=True,
                stop=True,
            )
            return bank

        y_pieces = [[(PACK, HALVES[0]), (0, HALVES[1])]] + [[(t, slice(0, S))] for t in range(1, PACK)]
        y_banks = [
            [(product(f"bank{number}", t, w1_codes, w1_scale, picked_codes, picked_scales, places), places) for number, places in pieces]
            for t, pieces in enumerate(y_pieces)
        ]
        deal(w2_codes, w2_raw, slice(0, PACK))
        w2_scale = sb("w2_scale", [P, H], U8)
        deal(w2_scale, w2_scale_rows, slice(0, PACK))

        y_plain = sb("y_plain", [P, PACK, S], F32)
        y_win = [sb(f"y_win{t}", [P, WINDOW], F32) for t in range(PACK)]
        gained_y = sb("gained_y", [P, PACK, S], F32)
        for t in range(PACK):
            copies = (y_plain[:, t, :], y_win[t][:, :S])
            for copy_of_y in copies if t < PACK - 1 else reversed(copies):
                for bank, places in y_banks[t]:
                    nc.scalar.copy(copy_of_y[:, places], bank[:])
        for t in range(PACK):
            for bank, places in y_banks[t]:
                nc.scalar.activation(gained_y[:, t, places], bank[:], ACT.Copy, scale=gain[:, t : t + 1])

        tab_less_y = sb("tab_less_y", [P, PACK, S], F32)
        st_win = [sb(f"st_win{t}", [P, WINDOW], F32) for t in range(PACK)]
        gate = sb("gate", [P, PACK, S], F32)
        size = sb("size", [P, PACK, S], F32)
        z2 = sb("z2", [P, PACK, S], F32)

        def differences(t):
            nc.vector.tensor_tensor(tab_less_y[:, t, :], tab_win[t][:].indirect(n3_sb[:]), y_plain[:, t, :], ALU.subtract)
            nc.vector.tensor_tensor(st_win[t][:, :S], y_win[t][:].indirect(n1_sb[:]), y_plain[:, t, :], ALU.subtract)
            nc.scalar.activation(gate[:, t, :], st_win[t][:].indirect(n2_sb[:]), ACT.Sigmoid)

        def z2_plane(t, tag):
            diff = sb(f"diff{t}", [P, S], F32, tag=tag)
            nc.vector.tensor_tensor(diff[:], y_win[t][:].indirect(n4_sb[:]), tab_less_y[:, t, :], ALU.add)
            nc.scalar.activation(size[:, t, :], diff[:], ACT.Abs)
            nc.scalar.activation(z2[:, t, :], size[:, t, :], ACT.Copy, scale=gain[:, t : t + 1])

        for t in range(PACK - 2):
            differences(t)
            z2_plane(t, None)
        differences(2)
        differences(3)
        z2_plane(2, "tab_win3")
        z2_plane(3, None)

        def quantize(name, packed):
            codes = sb(name + "_codes", [P, S], U32)
            scales = sb(name + "_scales", [P, S], U8)
            for cols in HALVES:
                nc.vector.quantize_mx(out=codes[:, cols].bitcast(FP8X4), scales=scales[:, cols], in_=packed[:, packed_cols(cols)])
            return codes, scales

        z_packed = sb("z_packed", [P, PACK * S], BF16)
        for cols in HALVES:
            nc.vector.tensor_tensor(side_by_side(z_packed, cols), by_planes(gate, cols), by_planes(gained_y, cols), ALU.mult)
        z_codes, z_scales = quantize("z", z_packed)
        z2_packed = sb("z2_packed", [P, PACK * S], BF16)
        nc.scalar.copy(side_by_side(z2_packed, HALVES[0]), by_planes(z2, HALVES[0]))
        nc.vector.tensor_copy(side_by_side(z2_packed, HALVES[1]), by_planes(z2, HALVES[1]))
        z2_codes, z2_scales = quantize("z2", z2_packed)

        result = [sb(f"result{t}", [P, S], F32) for t in range(PACK)]
        b_win = [sb(f"b_win{t}", [P, S], F32) for t in range(PACK)]
        half_a = sb("half_a", [P, PACK, W], F32)
        picked_b = sb("picked_b", [P, PACK, W], F32)
        out_rows = out_0.rearrange("(p t) j -> p t j", t=PACK)
        out_packed = sb("out_packed", [P, PACK * S], BF16)
        out_slots = out_packed[:].rearrange("p (c t) -> p t c", t=PACK)

        def make_a(t):
            pieces = [(PACK + t, slice(0, S))] if t > 0 else [(PACK - 1, HALVES[0]), (PACK, HALVES[1])]
            for number, places in pieces:
                bank = product(f"bank{number}", t, w2_codes, w2_scale, z_codes, z_scales, places)
                nc.scalar.copy(result[t][:, places], bank[:])

        def make_b(t):
            bank = product(f"bank{t}", t, w2_codes, w2_scale, z2_codes, z2_scales)
            nc.scalar.activation(b_win[t][:], bank[:], ACT.Copy, scale=-2.0)

        def fetch_a(t):
            nc.vector.tensor_copy(half_a[:, t, :], result[t][:].indirect(n5_sb[:]))

        def fetch_b(t):
            nc.vector.tensor_tensor(picked_b[:, t, :], b_win[t][:].indirect(n6_sb[:]), half_a[:, t, :], ALU.add)

        def put_back(t):
            nc.vector.tensor_tensor(result[t][:].indirect(n5_sb[:]), picked_b[:, t, :], minus_half[:], ALU.mult)
            nc.sync.dma_start(out=out_rows[:, t, :], in_=result[t][:])
            scalar_cols = slice(0, S) if t < 2 else HALVES[1]
            nc.scalar.copy(out_slots[:, t, scalar_cols], result[t][:, scalar_cols])

        for t in range(PACK):
            make_a(t)
            fetch_a(t)
        for t in range(PACK):
            make_b(t)
        for t in range(PACK):
            fetch_b(t)
            if t > 0:
                put_back(t - 1)
        put_back(PACK - 1)
        for t in (2, 3):
            nc.vector.tensor_copy(out_slots[:, t, HALVES[0]], result[t][:, HALVES[0]])

        out_codes, out_scales = quantize("out", out_packed)
        for cols, queue in zip(HALVES, (nc.sync, nc.scalar)):
            queue.dma_start(out=as_words(out_1)[:, cols], in_=out_codes[:, cols].bitcast(I32))
        for q in range(4):
            queue = nc.scalar if q % 2 else nc.sync
            queue.dma_start(out=out_2[0, 4 * q : 4 * q + 4, :].bitcast(I32), in_=out_scales[32 * q : 32 * q + 4, :].bitcast(I32))
